import numpy as np
import ml_dtypes

BF16 = ml_dtypes.bfloat16


def bf(x):
    return np.asarray(x, np.float32).astype(BF16)


def f32(x):
    return np.asarray(x, np.float32)


def f64(x):
    return np.asarray(x).astype(np.float64)


def striped(idx):
    return np.tile(idx.reshape(-1, 16).T, (8, 1))


def rows(idx, k):
    return np.tile(idx, (k, 1))


def look(tab, idx):
    return np.take_along_axis(f64(tab), rows(idx, len(tab)), axis=1)


K, S, V, N, M = 256, 4096, 2048, 2048, 256


def setup_inputs():
    return {"tab": f32(np.random.standard_normal((K, S))), "s": f32(np.random.uniform(0.5, 1.5, (K, 1))), "c": f32(0.3 * np.random.standard_normal((K, 1))), "w": bf(np.random.standard_normal((K, M)) / np.sqrt(K)), "b": f32(0.5 * np.random.standard_normal((M, 1))), "offs": striped(np.random.randint(0, S, N))}


def reference(tab, s, c, w, b, offs):
    idx = offs[:16].T.reshape(-1)
    t = look(tab, idx)
    x = f64(s) * t + f64(c)
    y = f64(w).T @ x
    return np.maximum(y + f64(b), 0.0)

@@ -1,0 +1,71 @@
+import concourse.mybir as mybir
+
+F32, BF16, U16 = mybir.dt.float32, mybir.dt.bfloat16, mybir.dt.uint16
+MULT, ADD = mybir.AluOpType.mult, mybir.AluOpType.add
+RELU = mybir.ActivationFunctionType.Relu
+
+P = 128
+R, S = 256, 4096
+N = 2048
+M = 256
+ROW_BLOCKS = R // P
+OUT_BLOCKS = M // P
+PIECE = 512
+PIECES = N // PIECE
+
+FLOPS = 2 * R * M * N + 2 * R * N + 2 * M * N
+
+
+def tile_lookup_deq_affp_relu_kernel(tc, tab, s, c, w, b, offs, out):
+    nc = tc.nc
+    with (
+        tc.tile_pool(name="held", bufs=1) as held,
+        tc.tile_pool(name="looked_up", bufs=4) as looked_up_pool,
+        tc.tile_pool(name="rounded", bufs=4) as rounded_pool,
+        tc.tile_pool(name="result", bufs=8) as result_pool,
+        tc.psum_pool(name="sums", bufs=1) as sums_pool,
+    ):
+        offsets = held.tile([P, N // 16], U16, name="offsets")
+        nc.sync.dma_start(offsets[:], offs)
+        windows = []
+        for r in range(ROW_BLOCKS):
+            window = held.tile([P, S], F32, name=f"window{r}")
+            nc.sync.dma_start(window[:], tab[r * P : (r + 1) * P, :])
+            windows.append(window)
+
+        scale = held.tile([P, ROW_BLOCKS], F32, name="scale")
+        shift = held.tile([P, ROW_BLOCKS], F32, name="shift")
+        bias = held.tile([P, OUT_BLOCKS], F32, name="bias")
+        with nc.allow_non_contiguous_dma(reason="one value a partition, 1 KiB in all"):
+            for vector_tile, vector in ((scale, s), (shift, c), (bias, b)):
+                nc.scalar.dma_start(vector_tile[:], vector.rearrange("(k p) o -> p (k o)", p=P))
+        weights = held.tile([P, ROW_BLOCKS, M], BF16, name="weights")
+        nc.scalar.dma_start(weights[:], w.rearrange("(k p) m -> p k m", p=P))
+
+        sums = [
+            [sums_pool.tile([P, PIECE], F32, name=f"sum_{m}_{j}") for j in range(PIECES)]
+            for m in range(OUT_BLOCKS)
+        ]
+        for r in range(ROW_BLOCKS):
+            for j in range(PIECES):
+                piece = offsets[:, j * (PIECE // 16) : (j + 1) * (PIECE // 16)]
+                x = looked_up_pool.tile([P, PIECE], F32, name="x")
+                nc.vector.tensor_scalar(
+                    x[:], windows[r][:].indirect(piece), scale[:, r : r + 1], shift[:, r : r + 1], MULT, ADD
+                )
+                x_rounded = rounded_pool.tile([P, PIECE], BF16, name="x_rounded")
+                nc.scalar.copy(x_rounded[:], x[:])
+                for m in range(OUT_BLOCKS):
+                    nc.tensor.matmul(
+                        sums[m][j][:],
+                        weights[:, r, m * P : (m + 1) * P],
+                        x_rounded[:],
+                        start=(r == 0),
+                        stop=(r == ROW_BLOCKS - 1),
+                    )
+                    if r == ROW_BLOCKS - 1:
+                        result = result_pool.tile([P, PIECE], F32, name="result")
+                        nc.scalar.activation(result[:], sums[m][j][:], RELU, bias=bias[:, m : m + 1])
+                        nc.sync.dma_start(
+                            out[m * P : (m + 1) * P, j * PIECE : (j + 1) * PIECE], result[:]
+                        )

@@ -54,7 +54,7 @@ def tile_lookup_deq_affp_relu_kernel(tc, tab, s, c, w, b, offs, out):
                     x[:], windows[r][:].indirect(piece), scale[:, r : r + 1], shift[:, r : r + 1], MULT, ADD
                 )
                 x_rounded = rounded_pool.tile([P, PIECE], BF16, name="x_rounded")
-                nc.scalar.copy(x_rounded[:], x[:])
+                nc.gpsimd.tensor_scalar(x_rounded[:], x[:], 1.0, None, MULT)
                 for m in range(OUT_BLOCKS):
                     nc.tensor.matmul(
                         sums[m][j][:],

@@ -1,7 +1,7 @@
 import concourse.mybir as mybir
 
 F32, BF16, U16 = mybir.dt.float32, mybir.dt.bfloat16, mybir.dt.uint16
-MULT, ADD = mybir.AluOpType.mult, mybir.AluOpType.add
+MULT, ADD, MAX = mybir.AluOpType.mult, mybir.AluOpType.add, mybir.AluOpType.max
 RELU = mybir.ActivationFunctionType.Relu
 
 P = 128
@@ -27,11 +27,11 @@ def tile_lookup_deq_affp_relu_kernel(tc, tab, s, c, w, b, offs, out):
     ):
         offsets = held.tile([P, N // 16], U16, name="offsets")
         nc.sync.dma_start(offsets[:], offs)
-        windows = []
-        for r in range(ROW_BLOCKS):
-            window = held.tile([P, S], F32, name=f"window{r}")
-            nc.sync.dma_start(window[:], tab[r * P : (r + 1) * P, :])
-            windows.append(window)
+        windows = [held.tile([P, S], F32, name=f"window{r}") for r in range(ROW_BLOCKS)]
+        weights = held.tile([P, ROW_BLOCKS, M], BF16, name="weights")
+        nc.sync.dma_start(windows[0][:], tab[:P, :])
+        nc.sync.dma_start(weights[:], w.rearrange("(k p) m -> p k m", p=P))
+        nc.sync.dma_start(windows[1][:], tab[P:, :])
 
         scale = held.tile([P, ROW_BLOCKS], F32, name="scale")
         shift = held.tile([P, ROW_BLOCKS], F32, name="shift")
@@ -39,33 +39,43 @@ def tile_lookup_deq_affp_relu_kernel(tc, tab, s, c, w, b, offs, out):
         with nc.allow_non_contiguous_dma(reason="one value a partition, 1 KiB in all"):
             for vector_tile, vector in ((scale, s), (shift, c), (bias, b)):
                 nc.scalar.dma_start(vector_tile[:], vector.rearrange("(k p) o -> p (k o)", p=P))
-        weights = held.tile([P, ROW_BLOCKS, M], BF16, name="weights")
-        nc.scalar.dma_start(weights[:], w.rearrange("(k p) m -> p k m", p=P))
 
         sums = [
             [sums_pool.tile([P, PIECE], F32, name=f"sum_{m}_{j}") for j in range(PIECES)]
             for m in range(OUT_BLOCKS)
         ]
-        for r in range(ROW_BLOCKS):
-            for j in range(PIECES):
-                piece = offsets[:, j * (PIECE // 16) : (j + 1) * (PIECE // 16)]
-                x = looked_up_pool.tile([P, PIECE], F32, name="x")
-                nc.vector.tensor_scalar(
-                    x[:], windows[r][:].indirect(piece), scale[:, r : r + 1], shift[:, r : r + 1], MULT, ADD
+
+        def look_up_and_multiply(r, j):
+            piece = offsets[:, j * (PIECE // 16) : (j + 1) * (PIECE // 16)]
+            x = looked_up_pool.tile([P, PIECE], F32, name="x")
+            nc.vector.tensor_scalar(
+                x[:], windows[r][:].indirect(piece), scale[:, r : r + 1], shift[:, r : r + 1], MULT, ADD
+            )
+            x_rounded = rounded_pool.tile([P, PIECE], BF16, name="x_rounded")
+            nc.scalar.copy(x_rounded[:], x[:])
+            for m in range(OUT_BLOCKS):
+                nc.tensor.matmul(
+                    sums[m][j][:],
+                    weights[:, r, m * P : (m + 1) * P],
+                    x_rounded[:],
+                    start=(r == 0),
+                    stop=(r == ROW_BLOCKS - 1),
                 )
-                x_rounded = rounded_pool.tile([P, PIECE], BF16, name="x_rounded")
-                nc.gpsimd.tensor_scalar(x_rounded[:], x[:], 1.0, None, MULT)
-                for m in range(OUT_BLOCKS):
-                    nc.tensor.matmul(
-                        sums[m][j][:],
-                        weights[:, r, m * P : (m + 1) * P],
-                        x_rounded[:],
-                        start=(r == 0),
-                        stop=(r == ROW_BLOCKS - 1),
-                    )
-                    if r == ROW_BLOCKS - 1:
-                        result = result_pool.tile([P, PIECE], F32, name="result")
-                        nc.scalar.activation(result[:], sums[m][j][:], RELU, bias=bias[:, m : m + 1])
-                        nc.sync.dma_start(
-                            out[m * P : (m + 1) * P, j * PIECE : (j + 1) * PIECE], result[:]
-                        )
+
+        def finish(m, j, on_vector):
+            result = result_pool.tile([P, PIECE], F32, name="result")
+            if on_vector:
+                nc.vector.tensor_scalar(result[:], sums[m][j][:], bias[:, m : m + 1], 0.0, ADD, MAX)
+            else:
+                nc.scalar.activation(result[:], sums[m][j][:], RELU, bias=bias[:, m : m + 1])
+            nc.sync.dma_start(out[m * P : (m + 1) * P, j * PIECE : (j + 1) * PIECE], result[:])
+
+        for j in range(PIECES):
+            look_up_and_multiply(0, j)
+        for j in range(PIECES):
+            look_up_and_multiply(1, j)
+            if j > 0:
+                finish(0, j - 1, on_vector=False)
+        finish(0, PIECES - 1, on_vector=False)
+        for j in range(PIECES):
+            finish(1, j, on_vector=True)

@@ -1,4 +1,5 @@
 import concourse.mybir as mybir
+from concourse.masks import make_identity
 
 F32, BF16, U16 = mybir.dt.float32, mybir.dt.bfloat16, mybir.dt.uint16
 MULT, ADD, MAX = mybir.AluOpType.mult, mybir.AluOpType.add, mybir.AluOpType.max
@@ -27,18 +28,23 @@ def tile_lookup_deq_affp_relu_kernel(tc, tab, s, c, w, b, offs, out):
     ):
         offsets = held.tile([P, N // 16], U16, name="offsets")
         nc.sync.dma_start(offsets[:], offs)
+        rows = held.tile([P, P], F32, name="rows")
+        nc.vector.memset(rows[:], 0.0)
+        for i, vector in enumerate((s, c, b)):
+            nc.sync.dma_start(rows[2 * i : 2 * i + 2, :], vector.rearrange("(k p) o -> k (p o)", p=P))
         windows = [held.tile([P, S], F32, name=f"window{r}") for r in range(ROW_BLOCKS)]
         weights = held.tile([P, ROW_BLOCKS, M], BF16, name="weights")
         nc.sync.dma_start(windows[0][:], tab[:P, :])
         nc.sync.dma_start(weights[:], w.rearrange("(k p) m -> p k m", p=P))
         nc.sync.dma_start(windows[1][:], tab[P:, :])
 
-        scale = held.tile([P, ROW_BLOCKS], F32, name="scale")
-        shift = held.tile([P, ROW_BLOCKS], F32, name="shift")
-        bias = held.tile([P, OUT_BLOCKS], F32, name="bias")
-        with nc.allow_non_contiguous_dma(reason="one value a partition, 1 KiB in all"):
-            for vector_tile, vector in ((scale, s), (shift, c), (bias, b)):
-                nc.scalar.dma_start(vector_tile[:], vector.rearrange("(k p) o -> p (k o)", p=P))
+        identity = held.tile([P, P], F32, name="identity")
+        make_identity(nc, identity[:])
+        turned = sums_pool.tile([P, P], F32, name="turned", tag=f"sum_{OUT_BLOCKS - 1}_{PIECES - 1}")
+        nc.tensor.transpose(turned[:], rows[:], identity[:])
+        columns = held.tile([P, 6], F32, name="columns")
+        nc.vector.tensor_copy(columns[:], turned[:, 0:6])
+        scale, shift, bias = columns[:, 0:2], columns[:, 2:4], columns[:, 4:6]
 
         sums = [
             [sums_pool.tile([P, PIECE], F32, name=f"sum_{m}_{j}") for j in range(PIECES)]
@@ -52,7 +58,10 @@ def tile_lookup_deq_affp_relu_kernel(tc, tab, s, c, w, b, offs, out):
                 x[:], windows[r][:].indirect(piece), scale[:, r : r + 1], shift[:, r : r + 1], MULT, ADD
             )
             x_rounded = rounded_pool.tile([P, PIECE], BF16, name="x_rounded")
-            nc.scalar.copy(x_rounded[:], x[:])
+            if r == ROW_BLOCKS - 1 and j == PIECES - 1:
+                nc.vector.tensor_copy(x_rounded[:], x[:])
+            else:
+                nc.scalar.copy(x_rounded[:], x[:])
             for m in range(OUT_BLOCKS):
                 nc.tensor.matmul(
                     sums[m][j][:],
@@ -76,6 +85,7 @@ def tile_lookup_deq_affp_relu_kernel(tc, tab, s, c, w, b, offs, out):
             look_up_and_multiply(1, j)
             if j > 0:
                 finish(0, j - 1, on_vector=False)
+        finish(1, 0, on_vector=False)
         finish(0, PIECES - 1, on_vector=False)
-        for j in range(PIECES):
+        for j in range(1, PIECES):
             finish(1, j, on_vector=True)

@@ -1,5 +1,4 @@
 import concourse.mybir as mybir
-from concourse.masks import make_identity
 
 F32, BF16, U16 = mybir.dt.float32, mybir.dt.bfloat16, mybir.dt.uint16
 MULT, ADD, MAX = mybir.AluOpType.mult, mybir.AluOpType.add, mybir.AluOpType.max
@@ -11,8 +10,11 @@ N = 2048
 M = 256
 ROW_BLOCKS = R // P
 OUT_BLOCKS = M // P
-PIECE = 512
-PIECES = N // PIECE
+BANK = 512
+BANKS = N // BANK
+HALF = BANK // 2
+PIECES = [(k * BANK, BANK) for k in range(BANKS)]
+LAST_PIECES = PIECES[:-1] + [(N - BANK, HALF), (N - HALF, HALF)]
 
 FLOPS = 2 * R * M * N + 2 * R * N + 2 * M * N
 
@@ -28,64 +30,63 @@ def tile_lookup_deq_affp_relu_kernel(tc, tab, s, c, w, b, offs, out):
     ):
         offsets = held.tile([P, N // 16], U16, name="offsets")
         nc.sync.dma_start(offsets[:], offs)
-        rows = held.tile([P, P], F32, name="rows")
-        nc.vector.memset(rows[:], 0.0)
-        for i, vector in enumerate((s, c, b)):
-            nc.sync.dma_start(rows[2 * i : 2 * i + 2, :], vector.rearrange("(k p) o -> k (p o)", p=P))
         windows = [held.tile([P, S], F32, name=f"window{r}") for r in range(ROW_BLOCKS)]
         weights = held.tile([P, ROW_BLOCKS, M], BF16, name="weights")
         nc.sync.dma_start(windows[0][:], tab[:P, :])
         nc.sync.dma_start(weights[:], w.rearrange("(k p) m -> p k m", p=P))
         nc.sync.dma_start(windows[1][:], tab[P:, :])
 
-        identity = held.tile([P, P], F32, name="identity")
-        make_identity(nc, identity[:])
-        turned = sums_pool.tile([P, P], F32, name="turned", tag=f"sum_{OUT_BLOCKS - 1}_{PIECES - 1}")
-        nc.tensor.transpose(turned[:], rows[:], identity[:])
-        columns = held.tile([P, 6], F32, name="columns")
-        nc.vector.tensor_copy(columns[:], turned[:, 0:6])
-        scale, shift, bias = columns[:, 0:2], columns[:, 2:4], columns[:, 4:6]
+        scale = held.tile([P, ROW_BLOCKS], F32, name="scale")
+        shift = held.tile([P, ROW_BLOCKS], F32, name="shift")
+        bias = held.tile([P, OUT_BLOCKS], F32, name="bias")
+        with nc.allow_non_contiguous_dma(reason="one value a partition, 1 KiB in all"):
+            for vector_tile, vector in ((scale, s), (shift, c), (bias, b)):
+                nc.scalar.dma_start(vector_tile[:], vector.rearrange("(k p) o -> p (k o)", p=P))
 
         sums = [
-            [sums_pool.tile([P, PIECE], F32, name=f"sum_{m}_{j}") for j in range(PIECES)]
+            [sums_pool.tile([P, BANK], F32, name=f"sum_{m}_{k}") for k in range(BANKS)]
             for m in range(OUT_BLOCKS)
         ]
 
-        def look_up_and_multiply(r, j):
-            piece = offsets[:, j * (PIECE // 16) : (j + 1) * (PIECE // 16)]
-            x = looked_up_pool.tile([P, PIECE], F32, name="x")
+        def sum_of(m, start, width):
+            first = start % BANK
+            return sums[m][start // BANK][:, first : first + width]
+
+        def look_up_and_multiply(r, start, width, on_vector):
+            piece = offsets[:, start // 16 : (start + width) // 16]
+            x = looked_up_pool.tile([P, width], F32, name="x")
             nc.vector.tensor_scalar(
                 x[:], windows[r][:].indirect(piece), scale[:, r : r + 1], shift[:, r : r + 1], MULT, ADD
             )
-            x_rounded = rounded_pool.tile([P, PIECE], BF16, name="x_rounded")
-            if r == ROW_BLOCKS - 1 and j == PIECES - 1:
+            x_rounded = rounded_pool.tile([P, width], BF16, name="x_rounded")
+            if on_vector:
                 nc.vector.tensor_copy(x_rounded[:], x[:])
             else:
                 nc.scalar.copy(x_rounded[:], x[:])
             for m in range(OUT_BLOCKS):
                 nc.tensor.matmul(
-                    sums[m][j][:],
+                    sum_of(m, start, width),
                     weights[:, r, m * P : (m + 1) * P],
                     x_rounded[:],
                     start=(r == 0),
-                    stop=(r == ROW_BLOCKS - 1),
+                    stop=(r == ROW_BLOCKS - 1 and (start + width) % BANK == 0),
                 )
 
-        def finish(m, j, on_vector):
-            result = result_pool.tile([P, PIECE], F32, name="result")
+        def finish(m, start, width, on_vector):
+            result = result_pool.tile([P, width], F32, name="result")
             if on_vector:
-                nc.vector.tensor_scalar(result[:], sums[m][j][:], bias[:, m : m + 1], 0.0, ADD, MAX)
+                nc.vector.tensor_scalar(result[:], sum_of(m, start, width), bias[:, m : m + 1], 0.0, ADD, MAX)
             else:
-                nc.scalar.activation(result[:], sums[m][j][:], RELU, bias=bias[:, m : m + 1])
-            nc.sync.dma_start(out[m * P : (m + 1) * P, j * PIECE : (j + 1) * PIECE], result[:])
+                nc.scalar.activation(result[:], sum_of(m, start, width), RELU, bias=bias[:, m : m + 1])
+            nc.sync.dma_start(out[m * P : (m + 1) * P, start : start + width], result[:])
 
-        for j in range(PIECES):
-            look_up_and_multiply(0, j)
-        for j in range(PIECES):
-            look_up_and_multiply(1, j)
-            if j > 0:
-                finish(0, j - 1, on_vector=False)
-        finish(1, 0, on_vector=False)
-        finish(0, PIECES - 1, on_vector=False)
-        for j in range(1, PIECES):
-            finish(1, j, on_vector=True)
+        for piece in PIECES:
+            look_up_and_multiply(0, *piece, on_vector=False)
+        for i, piece in enumerate(LAST_PIECES):
+            look_up_and_multiply(1, *piece, on_vector=(i == len(LAST_PIECES) - 1))
+            if i == 1:
+                finish(0, *PIECES[0], on_vector=False)
+        finish(1, *PIECES[0], on_vector=False)
+        for piece in PIECES[1:]:
+            finish(0, *piece, on_vector=False)
+            finish(1, *piece, on_vector=True)

import concourse.mybir as mybir

F32, BF16, U16 = mybir.dt.float32, mybir.dt.bfloat16, mybir.dt.uint16
MULT, ADD, MAX = mybir.AluOpType.mult, mybir.AluOpType.add, mybir.AluOpType.max
RELU = mybir.ActivationFunctionType.Relu

P = 128
R, S = 256, 4096
N = 2048
M = 256
ROW_BLOCKS = R // P
OUT_BLOCKS = M // P
BANK = 512
BANKS = N // BANK
HALF = BANK // 2
PIECES = [(k * BANK, BANK) for k in range(BANKS)]
LAST_PIECES = PIECES[:-1] + [(N - BANK, HALF), (N - HALF, HALF)]

FLOPS = 2 * R * M * N + 2 * R * N + 2 * M * N


def tile_lookup_deq_affp_relu_kernel(tc, tab, s, c, w, b, offs, out):
    nc = tc.nc
    with (
        tc.tile_pool(name="held", bufs=1) as held,
        tc.tile_pool(name="looked_up", bufs=4) as looked_up_pool,
        tc.tile_pool(name="rounded", bufs=4) as rounded_pool,
        tc.tile_pool(name="result", bufs=8) as result_pool,
        tc.psum_pool(name="sums", bufs=1) as sums_pool,
    ):
        offsets = held.tile([P, N // 16], U16, name="offsets")
        nc.sync.dma_start(offsets[:], offs)
        windows = [held.tile([P, S], F32, name=f"window{r}") for r in range(ROW_BLOCKS)]
        weights = held.tile([P, ROW_BLOCKS, M], BF16, name="weights")
        nc.sync.dma_start(windows[0][:], tab[:P, :])
        nc.sync.dma_start(weights[:], w.rearrange("(k p) m -> p k m", p=P))
        nc.sync.dma_start(windows[1][:], tab[P:, :])

        scale = held.tile([P, ROW_BLOCKS], F32, name="scale")
        shift = held.tile([P, ROW_BLOCKS], F32, name="shift")
        bias = held.tile([P, OUT_BLOCKS], F32, name="bias")
        with nc.allow_non_contiguous_dma(reason="one value a partition, 1 KiB in all"):
            for vector_tile, vector in ((scale, s), (shift, c), (bias, b)):
                nc.scalar.dma_start(vector_tile[:], vector.rearrange("(k p) o -> p (k o)", p=P))

        sums = [
            [sums_pool.tile([P, BANK], F32, name=f"sum_{m}_{k}") for k in range(BANKS)]
            for m in range(OUT_BLOCKS)
        ]

        def sum_of(m, start, width):
            first = start % BANK
            return sums[m][start // BANK][:, first : first + width]

        def look_up_and_multiply(r, start, width, on_vector):
            piece = offsets[:, start // 16 : (start + width) // 16]
            x = looked_up_pool.tile([P, width], F32, name="x")
            nc.vector.tensor_scalar(
                x[:], windows[r][:].indirect(piece), scale[:, r : r + 1], shift[:, r : r + 1], MULT, ADD
            )
            x_rounded = rounded_pool.tile([P, width], BF16, name="x_rounded")
            if on_vector:
                nc.vector.tensor_copy(x_rounded[:], x[:])
            else:
                nc.scalar.copy(x_rounded[:], x[:])
            for m in range(OUT_BLOCKS):
                nc.tensor.matmul(
                    sum_of(m, start, width),
                    weights[:, r, m * P : (m + 1) * P],
                    x_rounded[:],
                    start=(r == 0),
                    stop=(r == ROW_BLOCKS - 1 and (start + width) % BANK == 0),
                )

        def finish(m, start, width, on_vector):
            result = result_pool.tile([P, width], F32, name="result")
            if on_vector:
                nc.vector.tensor_scalar(result[:], sum_of(m, start, width), bias[:, m : m + 1], 0.0, ADD, MAX)
            else:
                nc.scalar.activation(result[:], sum_of(m, start, width), RELU, bias=bias[:, m : m + 1])
            nc.sync.dma_start(out[m * P : (m + 1) * P, start : start + width], result[:])

        for piece in PIECES:
            look_up_and_multiply(0, *piece, on_vector=False)
        for i, piece in enumerate(LAST_PIECES):
            look_up_and_multiply(1, *piece, on_vector=(i == len(LAST_PIECES) - 1))
            if i == 1:
                finish(0, *PIECES[0], on_vector=False)
        finish(1, *PIECES[0], on_vector=False)
        for piece in PIECES[1:]:
            finish(0, *piece, on_vector=False)
            finish(1, *piece, on_vector=True)
